import numpy as np
import ml_dtypes


def mxq(x, axis, fmt="e4m3"):
    dtype, down = {"e4m3": (ml_dtypes.float8_e4m3fn, 7), "e5m2": (ml_dtypes.float8_e5m2, 14)}[fmt]
    v = np.moveaxis(np.asarray(x, np.float32).astype(ml_dtypes.bfloat16).astype(np.float64), axis, -1)
    blocks = v.reshape(v.shape[:-1] + (-1, 32))
    amax = np.abs(blocks).max(-1, keepdims=True)
    byte = np.maximum(np.where(amax > 0, np.frexp(amax)[1] - 1 + 127, 0) - down, 1)
    scale = np.exp2(byte - 127.0)
    codes = (blocks / scale).astype(np.float32).astype(dtype).astype(np.float64)
    return np.moveaxis((codes * scale).reshape(v.shape), -1, axis)


WIDE = False


def mx_kscale(k):
    if not WIDE:
        return np.ones(k)
    levels = np.array([10, -10, 5, -5, 0])
    if k % 512:
        return np.exp2(np.random.permutation(np.resize(levels, k // 32))).repeat(32)
    a = np.empty((k // 512, 16))
    for p in range(k // 512):
        a[p, :8] = np.random.permutation(np.resize(levels, 8))
        for g in range(8):
            far = levels[np.abs(levels - a[p, g]) >= 10]
            a[p, g + 8] = far[np.random.randint(len(far))]
    return np.exp2(a.ravel()).repeat(32)


def f64(x):
    return np.asarray(x).astype(np.float64)


def striped(idx):
    return np.tile(idx.reshape(-1, 16).T, (8, 1)).astype(np.uint16)


def unstriped(offs):
    return offs[:16].T.reshape(-1).astype(np.int64)


def striped8(idx):
    return np.concatenate([x.reshape(-1, 16).T for x in idx]).astype(np.uint16)


def runs(offs, k):
    lists = np.stack([offs[16 * r : 16 * r + 16].T.reshape(-1) for r in range(8)]).astype(np.int64)
    return lists[np.arange(k) % 512 // 64]


def pack_weight(w):
    k, n = w.shape
    w = f64(np.asarray(w, np.float32).astype(ml_dtypes.bfloat16)).reshape(k // 32, 32, n)
    amax = np.abs(w).max(1)
    byte = np.clip(np.where(amax > 0, np.frexp(amax)[1] - 1 + 127 - 7, 1), 1, 254)
    scaled = (w * np.exp2(127.0 - byte)[:, None, :]).reshape(k, n).astype(np.float32)
    words = np.ascontiguousarray(scaled.reshape(k // 512, 128, 4, n).transpose(0, 1, 3, 2)).astype(ml_dtypes.float8_e4m3fn).view(np.uint8)
    return words, np.ascontiguousarray(byte.astype(np.uint8).reshape(k // 512, 16, n))


def unpack_weight(words, scales):
    g, p, n, _ = words.shape
    vals = np.ascontiguousarray(words).view(ml_dtypes.float8_e4m3fn).astype(np.float64) * np.repeat(np.exp2(scales.astype(np.float64) - 127.0), 8, axis=1)[..., None]
    return vals.transpose(0, 1, 3, 2).reshape(g * 512, n)

def planes(y):
    n, m = y.shape
    v = y.astype(np.float32).astype(ml_dtypes.bfloat16).astype(np.float64).reshape(n // 32, 32, m)
    top = np.abs(v).max(1)
    byte = np.clip(np.where(top > 0, np.frexp(top)[1] - 1 + 127 - 7, 1), 1, 254)
    codes = (v * np.exp2(127.0 - byte)[:, None, :]).reshape(n, m).astype(np.float32).astype(ml_dtypes.float8_e4m3fn).view(np.uint8)
    words = codes.reshape(n // 512, 128, 4, m).transpose(0, 1, 3, 2)
    return np.ascontiguousarray(words), np.ascontiguousarray(byte.astype(np.uint8).reshape(n // 512, 16, m))


K, T, S, G, H, J = 512, 1024, 512, 2048, 512, 512


def setup_inputs():
    n = np.random.standard_normal
    s = mx_kscale(K)[:, None]
    packed_xT = pack_weight(n((K, T)) * s)
    packed_dT = pack_weight(n((K, G)) / s)
    return {
        "x_words": packed_xT[0],
        "x_scales": packed_xT[1],
        "d_words": packed_dT[0],
        "d_scales": packed_dT[1],
        "gs": (np.random.uniform(0.5, 1.5, (K, 1)) * s).astype(np.float32),
        "tab": n((H, J)).astype(np.float32),
        "offs": striped(np.random.permutation(T)[:S]),
        "k1": striped8(np.random.randint(0, G, (8, H))),
        "n1": striped8(np.stack([np.random.permutation(S) for _ in range(8)])),
        "n2": striped8(np.stack([np.random.permutation(S) for _ in range(8)])),
        "k2": striped8(np.random.randint(0, G, (8, H))),
        "n3": striped8(np.random.randint(0, J, (8, S))),
        "n4": striped8(np.stack([np.random.permutation(S) for _ in range(8)])),
    }


def reference(x_words, x_scales, d_words, d_scales, gs, tab, offs, k1, n1, n2, k2, n3, n4):
    d_k2 = unpack_weight(d_words, d_scales)[np.arange(K)[:, None], runs(k2, K)]
    d_k1 = unpack_weight(d_words, d_scales)[np.arange(K)[:, None], runs(k1, K)]
    xq = unpack_weight(x_words, x_scales)[:, unstriped(offs)]
    h = 0.0625 * (d_k1.T @ xq)
    z = f64(gs) * ((h[np.arange(H)[:, None], runs(n1, H)]) * (h[np.arange(H)[:, None], runs(n2, H)]))
    h2 = 0.0625 * ((d_k2.T @ mxq(z, 0, "e4m3")))
    out_0 = np.abs(h2 - (h2[np.arange(H)[:, None], runs(n4, H)]) - (f64(tab)[np.arange(H)[:, None], runs(n3, H)]))
    return (out_0,) + planes(out_0)

@@ -1,0 +1,216 @@
+from contextlib import ExitStack
+
+import concourse.mybir as mybir
+
+K, T, S, G, H = 512, 1024, 512, 2048, 512
+FLOPS = 2 * (2 * K * H * S)
+
+F32 = mybir.dt.float32
+BF16 = mybir.dt.bfloat16
+I32 = mybir.dt.int32
+U32 = mybir.dt.uint32
+U16 = mybir.dt.uint16
+U8 = mybir.dt.uint8
+FP8X4 = mybir.dt.float8_e4m3fn_x4
+ALU = mybir.AluOpType
+ACT = mybir.ActivationFunctionType
+
+P = 128
+PACK = 4
+SIXTEENTH = 0.0625
+Z_PIECES = ((0, 256), (256, 128), (384, 128))
+TAB_PIECES = ((0, 256), (256, 256))
+OUT_PIECES = ((0, 256), (256, 128), (384, 128))
+
+
+def tile_picked_codeprodkindd_none_po_kernel(
+    tc, x_words, x_scales, d_words, d_scales, gs, tab, offs, k1, n1, n2, k2, n3, n4, out_0, out_1, out_2
+):
+    nc = tc.nc
+
+    with ExitStack() as ctx:
+        lists = ctx.enter_context(tc.tile_pool(name="lists", bufs=1))
+        shared = ctx.enter_context(tc.tile_pool(name="shared", bufs=1))
+        keep = ctx.enter_context(tc.tile_pool(name="keep", bufs=1))
+        psum = ctx.enter_context(tc.psum_pool(name="psum", bufs=1))
+
+        def load_list(source, name):
+            tile = lists.tile([P, S // 16], U16, name=name)
+            nc.sync.dma_start(tile[:], source)
+            return tile
+
+        def entries(tile, first, count):
+            return tile[:, first // 16 : (first + count) // 16]
+
+        d_bytes = keep.tile([P, G], U8, name="d_bytes")
+        x_bytes = keep.tile([P, T], U8, name="x_bytes")
+        placed = keep.tile([P, 3 * S], U8, name="placed", align_bytes=64)
+        nc.vector.memset(placed[:].bitcast(I32), 0)
+
+        def load_scale_rows(tile, source, width):
+            rows = source[0].bitcast(I32).unsqueeze(1).to_broadcast([16, 8, width // 4])
+            nc.sync.dma_start(tile[:].bitcast(I32), rows)
+
+        k1_list = load_list(k1, "k1_list")
+        load_scale_rows(d_bytes, d_scales, G)
+        k2_list = load_list(k2, "k2_list")
+        x_list = load_list(offs, "x_list")
+        load_scale_rows(x_bytes, x_scales, T)
+
+        gains = keep.tile([P, PACK], F32, name="gains")
+        nc.sync.dma_start(gains[:], gs.rearrange("(p t) o -> p (t o)", t=PACK))
+        x_table = keep.tile([P, T], U32, name="x_table")
+        nc.sync.dma_start(x_table[:].bitcast(I32), x_words[0].rearrange("p c r -> p (c r)").bitcast(I32))
+        d_table = shared.tile([P, G], U32, name="d_table", offset=0)
+        nc.sync.dma_start(d_table[:].bitcast(I32), d_words[0].rearrange("p c r -> p (c r)").bitcast(I32))
+
+        n1_list = load_list(n1, "n1_list")
+        n2_list = load_list(n2, "n2_list")
+        n3_list = load_list(n3, "n3_list")
+        n4_list = load_list(n4, "n4_list")
+        gains16 = keep.tile([P, PACK], F32, name="gains16")
+        nc.scalar.activation(gains16[:], gains[:], ACT.Copy, scale=SIXTEENTH)
+
+        picked_bytes = keep.tile([P, 3 * S], U8, name="picked_bytes", tag="reused")
+        nc.vector.tensor_copy(picked_bytes[:, 0:S], d_bytes[:].indirect(k1_list[:]))
+        nc.vector.tensor_copy(picked_bytes[:, S : 2 * S], d_bytes[:].indirect(k2_list[:]))
+        nc.vector.tensor_copy(picked_bytes[:, 2 * S : 3 * S], x_bytes[:].indirect(x_list[:]))
+        for q in range(4):
+            queue = nc.sync if q % 2 == 0 else nc.scalar
+            queue.dma_start(
+                placed[32 * q : 32 * q + 4, :].bitcast(I32),
+                picked_bytes[32 * q : 32 * q + 32 : 8, :].bitcast(I32),
+            )
+
+        x_picked = keep.tile([P, S], U32, name="x_picked", align_bytes=64)
+        nc.vector.tensor_copy(x_picked[:], x_table[:].indirect(x_list[:]))
+
+        def stationary(which, code_list, name, tag):
+            picked = keep.tile([P, H], U32, name=name + "_picked", tag=tag)
+            nc.vector.tensor_copy(picked[:], d_table[:].indirect(code_list[:]))
+            words = keep.tile([P, H], U32, name=name + "_words", align_bytes=64)
+            nc.vector.tensor_copy(
+                words[:].bitcast(I32).rearrange("p (t b i) -> p b t i", t=PACK, i=4),
+                picked[:].bitcast(I32).rearrange("p (b i t) -> p b t i", t=PACK, i=4),
+            )
+            scales = keep.tile([P, H], U8, name=name + "_scales", align_bytes=64)
+            nc.vector.tensor_copy(
+                scales[:].rearrange("p (t m) -> p t m", t=PACK),
+                placed[:, which * S : (which + 1) * S].rearrange("p (m t) -> p t m", t=PACK),
+            )
+            return words, scales
+
+        w1_words, w1_scales = stationary(0, k1_list, "w1", "w1_picked")
+
+        banks1 = [psum.tile([P, S], F32, name=f"bank1_{t}") for t in range(PACK)]
+        for t in range(PACK):
+            cols = slice(P * t, P * (t + 1))
+            nc.tensor.matmul_mx(
+                out=banks1[t][:],
+                lhsT=w1_words[:, cols].bitcast(FP8X4),
+                lhsT_scale=w1_scales[:, cols],
+                rhs=x_picked[:].bitcast(FP8X4),
+                rhs_scale=placed[:, 2 * S : 3 * S],
+                start=True,
+                stop=True,
+            )
+
+        w2_words, w2_scales = stationary(1, k2_list, "w2", "reused")
+
+        tabs = [shared.tile([P, S], F32, name=f"tab{t}", offset=4 * S * t) for t in range(PACK)]
+        tab_rows = tab.rearrange("(p t) j -> p t j", t=PACK)
+        for t in range(PACK):
+            nc.sync.dma_start(tabs[t][:], tab_rows[:, t, :])
+
+        h_gained = [keep.tile([P, S], F32, name=f"h_gained{t}") for t in range(PACK)]
+        h_plain = [keep.tile([P, S], F32, name=f"h_plain{t}") for t in range(PACK)]
+        for step in range(PACK + 1):
+            if step < PACK:
+                nc.scalar.activation(h_gained[step][:], banks1[step][:], ACT.Copy, scale=gains16[:, step : step + 1])
+            if step > 0:
+                nc.scalar.activation(h_plain[step - 1][:], banks1[step - 1][:], ACT.Copy, scale=SIXTEENTH)
+
+        def interleave(dst, src):
+            nc.scalar.copy(
+                dst.rearrange("p (c i) t -> p c t i", i=4),
+                src.rearrange("p t (c i) -> p c t i", i=4),
+            )
+
+        z_words = keep.tile([P, S], U32, name="z_words", align_bytes=64)
+        z_scales = keep.tile([P, S], U8, name="z_scales", align_bytes=64)
+        banks2 = [psum.tile([P, S], F32, name=f"bank2_{t}") for t in range(PACK)]
+        h2 = [keep.tile([P, S], F32, name=f"h2_{t}") for t in range(PACK)]
+        for first, count in Z_PIECES:
+            cols = slice(first, first + count)
+            left = keep.tile([P, PACK, count], F32, name=f"left{first}")
+            z = keep.tile([P, PACK, count], F32, name=f"z{first}")
+            for step in range(PACK + 1):
+                if step < PACK:
+                    nc.vector.tensor_copy(left[:, step, :], h_gained[step][:].indirect(entries(n1_list, first, count)))
+                if step > 0:
+                    t = step - 1
+                    nc.vector.tensor_tensor(
+                        z[:, t, :], h_plain[t][:].indirect(entries(n2_list, first, count)), left[:, t, :], ALU.mult
+                    )
+            z_rounded = keep.tile([P, count, PACK], BF16, name=f"z_rounded{first}", align_bytes=64)
+            interleave(z_rounded[:], z[:])
+            nc.vector.quantize_mx(
+                out=z_words[:, cols].bitcast(FP8X4),
+                scales=z_scales[:, cols],
+                in_=z_rounded[:].rearrange("p c t -> p (c t)"),
+            )
+            for t in range(PACK):
+                rows = slice(P * t, P * (t + 1))
+                nc.tensor.matmul_mx(
+                    out=banks2[t][:, cols],
+                    lhsT=w2_words[:, rows].bitcast(FP8X4),
+                    lhsT_scale=w2_scales[:, rows],
+                    rhs=z_words[:, cols].bitcast(FP8X4),
+                    rhs_scale=z_scales[:, cols],
+                    start=True,
+                    stop=True,
+                )
+                nc.scalar.activation(h2[t][:, cols], banks2[t][:, cols], ACT.Copy, scale=SIXTEENTH)
+
+        y_words = keep.tile([P, S], U32, name="y_words", align_bytes=64)
+        y_scales = keep.tile([P, S], U8, name="y_scales", align_bytes=64)
+        out_rows = out_0.rearrange("(p t) j -> p t j", t=PACK)
+        out_words = out_1[0].rearrange("p c r -> p (c r)").bitcast(I32)
+        for tab_first, tab_count in TAB_PIECES:
+            partial = keep.tile([P, PACK, tab_count], F32, name=f"partial{tab_first}")
+            for t in range(PACK):
+                nc.vector.tensor_tensor(
+                    partial[:, t, :],
+                    tabs[t][:].indirect(entries(n3_list, tab_first, tab_count)),
+                    h2[t][:, tab_first : tab_first + tab_count],
+                    ALU.subtract,
+                )
+            for first, count in OUT_PIECES:
+                if not tab_first <= first < tab_first + tab_count:
+                    continue
+                cols = slice(first, first + count)
+                signed = keep.tile([P, PACK, count], F32, name=f"signed{first}")
+                y = keep.tile([P, PACK, count], F32, name=f"y{first}")
+                for t in range(PACK):
+                    nc.vector.tensor_tensor(
+                        signed[:, t, :],
+                        h2[t][:].indirect(entries(n4_list, first, count)),
+                        partial[:, t, first - tab_first : first - tab_first + count],
+                        ALU.add,
+                    )
+                y_rounded = keep.tile([P, count, PACK], BF16, name=f"y_rounded{first}", align_bytes=64)
+                nc.scalar.activation(
+                    y_rounded[:].rearrange("p (c i) t -> p c t i", i=4),
+                    signed[:].rearrange("p t (c i) -> p c t i", i=4),
+                    ACT.Abs,
+                )
+                nc.scalar.activation(y[:], signed[:], ACT.Abs)
+                nc.scalar.dma_start(out_rows[:, :, cols], y[:])
+                nc.vector.quantize_mx(
+                    out=y_words[:, cols].bitcast(FP8X4),
+                    scales=y_scales[:, cols],
+                    in_=y_rounded[:].rearrange("p c t -> p (c t)"),
+                )
+                nc.sync.dma_start(out_words[:, cols], y_words[:, cols].bitcast(I32))
+        for q in range(4):
+            nc.sync.dma_start(out_2[0, 4 * q : 4 * q + 4, :].bitcast(I32), y_scales[32 * q : 32 * q + 4, :].bitcast(I32))

@@ -18,9 +18,9 @@ ACT = mybir.ActivationFunctionType
 P = 128
 PACK = 4
 SIXTEENTH = 0.0625
-Z_PIECES = ((0, 256), (256, 128), (384, 128))
-TAB_PIECES = ((0, 256), (256, 256))
-OUT_PIECES = ((0, 256), (256, 128), (384, 128))
+HALF = S // 2
+QUARTER = S // 4
+KIB = 1024
 
 
 def tile_picked_codeprodkindd_none_po_kernel(
@@ -30,7 +30,8 @@ def tile_picked_codeprodkindd_none_po_kernel(
 
     with ExitStack() as ctx:
         lists = ctx.enter_context(tc.tile_pool(name="lists", bufs=1))
-        shared = ctx.enter_context(tc.tile_pool(name="shared", bufs=1))
+        tables = ctx.enter_context(tc.tile_pool(name="tables", bufs=1))
+        turns = ctx.enter_context(tc.tile_pool(name="turns", bufs=1))
         keep = ctx.enter_context(tc.tile_pool(name="keep", bufs=1))
         psum = ctx.enter_context(tc.psum_pool(name="psum", bufs=1))
 
@@ -42,82 +43,93 @@ def tile_picked_codeprodkindd_none_po_kernel(
         def entries(tile, first, count):
             return tile[:, first // 16 : (first + count) // 16]
 
-        d_bytes = keep.tile([P, G], U8, name="d_bytes")
-        x_bytes = keep.tile([P, T], U8, name="x_bytes")
-        placed = keep.tile([P, 3 * S], U8, name="placed", align_bytes=64)
-        nc.vector.memset(placed[:].bitcast(I32), 0)
-
-        def load_scale_rows(tile, source, width):
+        def load_scale_rows(source, width, name):
+            tile = keep.tile([P, width], U8, name=name)
             rows = source[0].bitcast(I32).unsqueeze(1).to_broadcast([16, 8, width // 4])
             nc.sync.dma_start(tile[:].bitcast(I32), rows)
+            return tile
 
-        k1_list = load_list(k1, "k1_list")
-        load_scale_rows(d_bytes, d_scales, G)
-        k2_list = load_list(k2, "k2_list")
         x_list = load_list(offs, "x_list")
-        load_scale_rows(x_bytes, x_scales, T)
-
-        gains = keep.tile([P, PACK], F32, name="gains")
-        nc.sync.dma_start(gains[:], gs.rearrange("(p t) o -> p (t o)", t=PACK))
+        x_bytes = load_scale_rows(x_scales, T, "x_bytes")
+        k1_list = load_list(k1, "k1_list")
+        d_bytes = load_scale_rows(d_scales, G, "d_bytes")
         x_table = keep.tile([P, T], U32, name="x_table")
         nc.sync.dma_start(x_table[:].bitcast(I32), x_words[0].rearrange("p c r -> p (c r)").bitcast(I32))
-        d_table = shared.tile([P, G], U32, name="d_table", offset=0)
-        nc.sync.dma_start(d_table[:].bitcast(I32), d_words[0].rearrange("p c r -> p (c r)").bitcast(I32))
-
         n1_list = load_list(n1, "n1_list")
         n2_list = load_list(n2, "n2_list")
+        d_table = tables.tile([P, G], U32, name="d_table", offset=0)
+        nc.sync.dma_start(d_table[:].bitcast(I32), d_words[0].rearrange("p c r -> p (c r)").bitcast(I32))
         n3_list = load_list(n3, "n3_list")
         n4_list = load_list(n4, "n4_list")
+        k2_list = load_list(k2, "k2_list")
+        gains = keep.tile([P, PACK], F32, name="gains")
+        nc.sync.dma_start(gains[:], gs.rearrange("(p t) o -> p (t o)", t=PACK))
         gains16 = keep.tile([P, PACK], F32, name="gains16")
         nc.scalar.activation(gains16[:], gains[:], ACT.Copy, scale=SIXTEENTH)
 
-        picked_bytes = keep.tile([P, 3 * S], U8, name="picked_bytes", tag="reused")
-        nc.vector.tensor_copy(picked_bytes[:, 0:S], d_bytes[:].indirect(k1_list[:]))
-        nc.vector.tensor_copy(picked_bytes[:, S : 2 * S], d_bytes[:].indirect(k2_list[:]))
-        nc.vector.tensor_copy(picked_bytes[:, 2 * S : 3 * S], x_bytes[:].indirect(x_list[:]))
-        for q in range(4):
-            queue = nc.sync if q % 2 == 0 else nc.scalar
-            queue.dma_start(
-                placed[32 * q : 32 * q + 4, :].bitcast(I32),
-                picked_bytes[32 * q : 32 * q + 32 : 8, :].bitcast(I32),
+        def gather_bytes(table, code_list, name):
+            picked = keep.tile([P, S], U8, name=name)
+            nc.vector.tensor_copy(picked[:], table[:].indirect(code_list[:]))
+            return picked
+
+        def deal_bytes(dealt, picked):
+            nc.vector.tensor_copy(
+                dealt.rearrange("p (t m) -> p t m", t=PACK), picked[:].rearrange("p (m t) -> p t m", t=PACK)
             )
 
-        x_picked = keep.tile([P, S], U32, name="x_picked", align_bytes=64)
-        nc.vector.tensor_copy(x_picked[:], x_table[:].indirect(x_list[:]))
+        def place_rows(spread, width, name, queues):
+            placed = keep.tile([P, width], U8, name=name, align_bytes=64)
+            nc.vector.memset(placed[:].bitcast(I32), 0)
+            for q in range(4):
+                queues[q % len(queues)].dma_start(
+                    placed[32 * q : 32 * q + 4, :].bitcast(I32), spread[32 * q : 32 * q + 32 : 8, :].bitcast(I32)
+                )
+            return placed
 
-        def stationary(which, code_list, name, tag):
-            picked = keep.tile([P, H], U32, name=name + "_picked", tag=tag)
-            nc.vector.tensor_copy(picked[:], d_table[:].indirect(code_list[:]))
-            words = keep.tile([P, H], U32, name=name + "_words", align_bytes=64)
+        def gather_words(table, code_list, name):
+            picked = keep.tile([P, S], U32, name=name, align_bytes=64)
+            nc.vector.tensor_copy(picked[:], table[:].indirect(code_list[:]))
+            return picked
+
+        def deal_words(picked, name):
+            dealt = keep.tile([P, H], U32, name=name, align_bytes=64)
             nc.vector.tensor_copy(
-                words[:].bitcast(I32).rearrange("p (t b i) -> p b t i", t=PACK, i=4),
+                dealt[:].bitcast(I32).rearrange("p (t b i) -> p b t i", t=PACK, i=4),
                 picked[:].bitcast(I32).rearrange("p (b i t) -> p b t i", t=PACK, i=4),
             )
-            scales = keep.tile([P, H], U8, name=name + "_scales", align_bytes=64)
-            nc.vector.tensor_copy(
-                scales[:].rearrange("p (t m) -> p t m", t=PACK),
-                placed[:, which * S : (which + 1) * S].rearrange("p (m t) -> p t m", t=PACK),
-            )
-            return words, scales
+            return dealt
 
-        w1_words, w1_scales = stationary(0, k1_list, "w1", "w1_picked")
+        x_picked_bytes = gather_bytes(x_bytes, x_list, "x_picked_bytes")
+        w1_bytes = gather_bytes(d_bytes, k1_list, "w1_bytes")
+        spread1 = keep.tile([P, H + S], U8, name="spread1")
+        nc.vector.tensor_copy(spread1[:, H : H + S].bitcast(I32), x_picked_bytes[:].bitcast(I32))
+        deal_bytes(spread1[:, 0:H], w1_bytes)
+        scales1 = place_rows(spread1, H + S, "scales1", (nc.scalar, nc.sync))
+
+        x_picked = gather_words(x_table, x_list, "x_picked")
+        w1_words = deal_words(gather_words(d_table, k1_list, "w1_picked"), "w1_words")
 
         banks1 = [psum.tile([P, S], F32, name=f"bank1_{t}") for t in range(PACK)]
         for t in range(PACK):
-            cols = slice(P * t, P * (t + 1))
+            rows = slice(P * t, P * (t + 1))
             nc.tensor.matmul_mx(
                 out=banks1[t][:],
-                lhsT=w1_words[:, cols].bitcast(FP8X4),
-                lhsT_scale=w1_scales[:, cols],
+                lhsT=w1_words[:, rows].bitcast(FP8X4),
+                lhsT_scale=scales1[:, rows],
                 rhs=x_picked[:].bitcast(FP8X4),
-                rhs_scale=placed[:, 2 * S : 3 * S],
+                rhs_scale=scales1[:, H : H + S],
                 start=True,
                 stop=True,
             )
 
-        w2_words, w2_scales = stationary(1, k2_list, "w2", "reused")
+        w2_bytes = gather_bytes(d_bytes, k2_list, "w2_bytes")
+        w2_picked = gather_words(d_table, k2_list, "w2_picked")
+        spread2 = keep.tile([P, H], U8, name="spread2")
+        deal_bytes(spread2[:], w2_bytes)
+        w2_scales = place_rows(spread2, H, "w2_scales", (nc.sync,))
+        w2_words = deal_words(w2_picked, "w2_words")
 
-        tabs = [shared.tile([P, S], F32, name=f"tab{t}", offset=4 * S * t) for t in range(PACK)]
+        tabs = [tables.tile([P, S], F32, name=f"tab{t}", offset=4 * S * t) for t in range(PACK)]
         tab_rows = tab.rearrange("(p t) j -> p t j", t=PACK)
         for t in range(PACK):
             nc.sync.dma_start(tabs[t][:], tab_rows[:, t, :])
@@ -130,35 +142,35 @@ def tile_picked_codeprodkindd_none_po_kernel(
             if step > 0:
                 nc.scalar.activation(h_plain[step - 1][:], banks1[step - 1][:], ACT.Copy, scale=SIXTEENTH)
 
-        def interleave(dst, src):
-            nc.scalar.copy(
-                dst.rearrange("p (c i) t -> p c t i", i=4),
-                src.rearrange("p t (c i) -> p c t i", i=4),
-            )
-
         z_words = keep.tile([P, S], U32, name="z_words", align_bytes=64)
         z_scales = keep.tile([P, S], U8, name="z_scales", align_bytes=64)
         banks2 = [psum.tile([P, S], F32, name=f"bank2_{t}") for t in range(PACK)]
         h2 = [keep.tile([P, S], F32, name=f"h2_{t}") for t in range(PACK)]
-        for first, count in Z_PIECES:
-            cols = slice(first, first + count)
-            left = keep.tile([P, PACK, count], F32, name=f"left{first}")
-            z = keep.tile([P, PACK, count], F32, name=f"z{first}")
+
+        def gather_z(first, count, left, z):
             for step in range(PACK + 1):
                 if step < PACK:
-                    nc.vector.tensor_copy(left[:, step, :], h_gained[step][:].indirect(entries(n1_list, first, count)))
+                    nc.vector.tensor_copy(left[step], h_gained[step][:].indirect(entries(n1_list, first, count)))
                 if step > 0:
                     t = step - 1
                     nc.vector.tensor_tensor(
-                        z[:, t, :], h_plain[t][:].indirect(entries(n2_list, first, count)), left[:, t, :], ALU.mult
+                        z[:, t, :], h_plain[t][:].indirect(entries(n2_list, first, count)), left[t], ALU.mult
                     )
+
+        def quantise_z(first, count, z):
+            cols = slice(first, first + count)
             z_rounded = keep.tile([P, count, PACK], BF16, name=f"z_rounded{first}", align_bytes=64)
-            interleave(z_rounded[:], z[:])
+            nc.scalar.copy(
+                z_rounded[:].rearrange("p (c i) t -> p c t i", i=4), z.rearrange("p t (c i) -> p c t i", i=4)
+            )
             nc.vector.quantize_mx(
                 out=z_words[:, cols].bitcast(FP8X4),
                 scales=z_scales[:, cols],
                 in_=z_rounded[:].rearrange("p c t -> p (c t)"),
             )
+
+        def second_product(first):
+            cols = slice(first, first + HALF)
             for t in range(PACK):
                 rows = slice(P * t, P * (t + 1))
                 nc.tensor.matmul_mx(
@@ -172,45 +184,74 @@ def tile_picked_codeprodkindd_none_po_kernel(
                 )
                 nc.scalar.activation(h2[t][:, cols], banks2[t][:, cols], ACT.Copy, scale=SIXTEENTH)
 
+        most = S - QUARTER
+        z_rows = keep.tile([P, PACK + 2, most], F32, name="z_rows")
+        z_a = z_rows[:, 2 : PACK + 2, :]
+        left_a = [turns.tile([P, most], F32, name=f"left_a{t}", offset=(18 + 2 * t) * KIB) for t in range(PACK)]
+        gather_z(0, most, [tile[:] for tile in left_a], z_a)
+        quantise_z(0, HALF, z_a[:, :, 0:HALF])
+        second_product(0)
+        quantise_z(HALF, QUARTER, z_a[:, :, HALF:most])
+
+        z_c = z_rows[:, 0:PACK, 0:QUARTER]
+        left_c0 = turns.tile([P, QUARTER], F32, name="left_c0", offset=22 * KIB)
+        left_c12 = turns.tile([P, 2, QUARTER], F32, name="left_c12", offset=24 * KIB)
+        gather_z(most, QUARTER, [left_c0[:], left_c12[:, 0, :], left_c12[:, 1, :], z_rows[:, PACK, 0:QUARTER]], z_c)
+        quantise_z(most, QUARTER, z_c)
+        second_product(HALF)
+
         y_words = keep.tile([P, S], U32, name="y_words", align_bytes=64)
         y_scales = keep.tile([P, S], U8, name="y_scales", align_bytes=64)
         out_rows = out_0.rearrange("(p t) j -> p t j", t=PACK)
         out_words = out_1[0].rearrange("p c r -> p (c r)").bitcast(I32)
-        for tab_first, tab_count in TAB_PIECES:
-            partial = keep.tile([P, PACK, tab_count], F32, name=f"partial{tab_first}")
+
+        def tab_less_h2(first, partial):
             for t in range(PACK):
                 nc.vector.tensor_tensor(
-                    partial[:, t, :],
-                    tabs[t][:].indirect(entries(n3_list, tab_first, tab_count)),
-                    h2[t][:, tab_first : tab_first + tab_count],
+                    partial[t],
+                    tabs[t][:].indirect(entries(n3_list, first, HALF)),
+                    h2[t][:, first : first + HALF],
                     ALU.subtract,
                 )
-            for first, count in OUT_PIECES:
-                if not tab_first <= first < tab_first + tab_count:
-                    continue
-                cols = slice(first, first + count)
-                signed = keep.tile([P, PACK, count], F32, name=f"signed{first}")
-                y = keep.tile([P, PACK, count], F32, name=f"y{first}")
-                for t in range(PACK):
-                    nc.vector.tensor_tensor(
-                        signed[:, t, :],
-                        h2[t][:].indirect(entries(n4_list, first, count)),
-                        partial[:, t, first - tab_first : first - tab_first + count],
-                        ALU.add,
-                    )
-                y_rounded = keep.tile([P, count, PACK], BF16, name=f"y_rounded{first}", align_bytes=64)
-                nc.scalar.activation(
-                    y_rounded[:].rearrange("p (c i) t -> p c t i", i=4),
-                    signed[:].rearrange("p t (c i) -> p c t i", i=4),
-                    ACT.Abs,
+
+        def make_y(first, count, partial, signed, queue):
+            cols = slice(first, first + count)
+            y = keep.tile([P, PACK, count], F32, name=f"y{first}")
+            for t in range(PACK):
+                nc.vector.tensor_tensor(
+                    signed[:, t, :], h2[t][:].indirect(entries(n4_list, first, count)), partial[t], ALU.add
                 )
-                nc.scalar.activation(y[:], signed[:], ACT.Abs)
-                nc.scalar.dma_start(out_rows[:, :, cols], y[:])
-                nc.vector.quantize_mx(
-                    out=y_words[:, cols].bitcast(FP8X4),
-                    scales=y_scales[:, cols],
-                    in_=y_rounded[:].rearrange("p c t -> p (c t)"),
-                )
-                nc.sync.dma_start(out_words[:, cols], y_words[:, cols].bitcast(I32))
+                if t < PACK - 1:
+                    nc.scalar.activation(y[:, t, :], signed[:, t, :], ACT.Abs)
+            y_rounded = keep.tile([P, count, PACK], BF16, name=f"y_rounded{first}", align_bytes=64)
+            nc.scalar.activation(
+                y_rounded[:].rearrange("p (c i) t -> p c t i", i=4),
+                signed[:].rearrange("p t (c i) -> p c t i", i=4),
+                ACT.Abs,
+            )
+            nc.scalar.activation(y[:, PACK - 1, :], signed[:, PACK - 1, :], ACT.Abs)
+            queue.dma_start(out_rows[:, :, cols], y[:])
+            nc.vector.quantize_mx(
+                out=y_words[:, cols].bitcast(FP8X4),
+                scales=y_scales[:, cols],
+                in_=y_rounded[:].rearrange("p c t -> p (c t)"),
+            )
+
+        partial_a01 = keep.tile([P, 2, HALF], F32, name="partial_a01")
+        partial_a = [partial_a01[:, 0, :], partial_a01[:, 1, :], z_rows[:, 0, 0:HALF], z_rows[:, 1, 0:HALF]]
+        tab_less_h2(0, partial_a)
+        signed_a = turns.tile([P, PACK, HALF], F32, name="signed_a", offset=13 * KIB)
+        make_y(0, HALF, partial_a, signed_a, nc.sync)
+        nc.sync.dma_start(out_words[:, 0:HALF], y_words[:, 0:HALF].bitcast(I32))
+
+        z_flat = z_rows[:].rearrange("p r c -> p (r c)")
+        partial_b = [z_flat[:, HALF * t : HALF * (t + 1)] for t in range(PACK)]
+        tab_less_h2(HALF, partial_b)
+        signed_b = keep.tile([P, PACK, QUARTER], F32, name="signed_b")
+        make_y(HALF, QUARTER, [part[:, 0:QUARTER] for part in partial_b], signed_b, nc.sync)
+        signed_c = turns.tile([P, PACK, QUARTER], F32, name="signed_c", offset=13 * KIB)
+        make_y(HALF + QUARTER, QUARTER, [part[:, QUARTER:HALF] for part in partial_b], signed_c, nc.scalar)
+        nc.sync.dma_start(out_words[:, HALF:S], y_words[:, HALF:S].bitcast(I32))
         for q in range(4):
-            nc.sync.dma_start(out_2[0, 4 * q : 4 * q + 4, :].bitcast(I32), y_scales[32 * q : 32 * q + 4, :].bitcast(I32))
+            queue = nc.sync if q % 2 == 0 else nc.scalar
+            queue.dma_start(out_2[0, 4 * q : 4 * q + 4, :].bitcast(I32), y_scales[32 * q : 32 * q + 4, :].bitcast(I32))

@@ -46,7 +46,7 @@ def tile_picked_codeprodkindd_none_po_kernel(
         def load_scale_rows(source, width, name):
             tile = keep.tile([P, width], U8, name=name)
             rows = source[0].bitcast(I32).unsqueeze(1).to_broadcast([16, 8, width // 4])
-            nc.sync.dma_start(tile[:].bitcast(I32), rows)
+            nc.scalar.dma_start(tile[:].bitcast(I32), rows)
             return tile
 
         x_list = load_list(offs, "x_list")
@@ -214,7 +214,7 @@ def tile_picked_codeprodkindd_none_po_kernel(
                     ALU.subtract,
                 )
 
-        def make_y(first, count, partial, signed, queue):
+        def make_y(first, count, partial, signed, last):
             cols = slice(first, first + count)
             y = keep.tile([P, PACK, count], F32, name=f"y{first}")
             for t in range(PACK):
@@ -230,7 +230,15 @@ def tile_picked_codeprodkindd_none_po_kernel(
                 ACT.Abs,
             )
             nc.scalar.activation(y[:, PACK - 1, :], signed[:, PACK - 1, :], ACT.Abs)
-            queue.dma_start(out_rows[:, :, cols], y[:])
+            if last:
+                nc.sync.dma_start(out_rows[:, 0 : PACK - 1, cols], y[:, 0 : PACK - 1, :])
+                nc.scalar.dma_start(out_rows[:, PACK - 1, cols], y[:, PACK - 1, :])
+            else:
+                nc.sync.dma_start(out_rows[:, :, cols], y[:])
+            return y_rounded
+
+        def quantise_y(first, count, y_rounded):
+            cols = slice(first, first + count)
             nc.vector.quantize_mx(
                 out=y_words[:, cols].bitcast(FP8X4),
                 scales=y_scales[:, cols],
@@ -240,18 +248,21 @@ def tile_picked_codeprodkindd_none_po_kernel(
         partial_a01 = keep.tile([P, 2, HALF], F32, name="partial_a01")
         partial_a = [partial_a01[:, 0, :], partial_a01[:, 1, :], z_rows[:, 0, 0:HALF], z_rows[:, 1, 0:HALF]]
         tab_less_h2(0, partial_a)
-        signed_a = turns.tile([P, PACK, HALF], F32, name="signed_a", offset=13 * KIB)
-        make_y(0, HALF, partial_a, signed_a, nc.sync)
-        nc.sync.dma_start(out_words[:, 0:HALF], y_words[:, 0:HALF].bitcast(I32))
+        signed_a = keep.tile([P, PACK, HALF], F32, name="signed_a")
+        rounded_a = make_y(0, HALF, partial_a, signed_a, False)
 
         z_flat = z_rows[:].rearrange("p r c -> p (r c)")
         partial_b = [z_flat[:, HALF * t : HALF * (t + 1)] for t in range(PACK)]
         tab_less_h2(HALF, partial_b)
         signed_b = keep.tile([P, PACK, QUARTER], F32, name="signed_b")
-        make_y(HALF, QUARTER, [part[:, 0:QUARTER] for part in partial_b], signed_b, nc.sync)
-        signed_c = turns.tile([P, PACK, QUARTER], F32, name="signed_c", offset=13 * KIB)
-        make_y(HALF + QUARTER, QUARTER, [part[:, QUARTER:HALF] for part in partial_b], signed_c, nc.scalar)
-        nc.sync.dma_start(out_words[:, HALF:S], y_words[:, HALF:S].bitcast(I32))
+        rounded_b = make_y(HALF, QUARTER, [part[:, 0:QUARTER] for part in partial_b], signed_b, False)
+        signed_c = keep.tile([P, PACK, QUARTER], F32, name="signed_c")
+        rounded_c = make_y(HALF + QUARTER, QUARTER, [part[:, QUARTER:HALF] for part in partial_b], signed_c, True)
+        quantise_y(0, HALF, rounded_a)
+        quantise_y(HALF, QUARTER, rounded_b)
+        nc.sync.dma_start(out_words[:, 0:most], y_words[:, 0:most].bitcast(I32))
+        quantise_y(most, QUARTER, rounded_c)
+        nc.sync.dma_start(out_words[:, most:S], y_words[:, most:S].bitcast(I32))
         for q in range(4):
             queue = nc.sync if q % 2 == 0 else nc.scalar
             queue.dma_start(out_2[0, 4 * q : 4 * q + 4, :].bitcast(I32), y_scales[32 * q : 32 * q + 4, :].bitcast(I32))

@@ -17,10 +17,15 @@ ACT = mybir.ActivationFunctionType
 
 P = 128
 PACK = 4
+GROUP = 16
+BLOCK = 8
+QUADRANT = 32
+LINE = 4
 SIXTEENTH = 0.0625
 HALF = S // 2
 QUARTER = S // 4
-KIB = 1024
+MOST = S - QUARTER
+LEFT_BYTES = 2048
 
 
 def tile_picked_codeprodkindd_none_po_kernel(
@@ -31,21 +36,21 @@ def tile_picked_codeprodkindd_none_po_kernel(
     with ExitStack() as ctx:
         lists = ctx.enter_context(tc.tile_pool(name="lists", bufs=1))
         tables = ctx.enter_context(tc.tile_pool(name="tables", bufs=1))
-        turns = ctx.enter_context(tc.tile_pool(name="turns", bufs=1))
+        factors = ctx.enter_context(tc.tile_pool(name="factors", bufs=1))
         keep = ctx.enter_context(tc.tile_pool(name="keep", bufs=1))
         psum = ctx.enter_context(tc.psum_pool(name="psum", bufs=1))
 
         def load_list(source, name):
-            tile = lists.tile([P, S // 16], U16, name=name)
+            tile = lists.tile([P, S // GROUP], U16, name=name)
             nc.sync.dma_start(tile[:], source)
             return tile
 
         def entries(tile, first, count):
-            return tile[:, first // 16 : (first + count) // 16]
+            return tile[:, first // GROUP : (first + count) // GROUP]
 
         def load_scale_rows(source, width, name):
             tile = keep.tile([P, width], U8, name=name)
-            rows = source[0].bitcast(I32).unsqueeze(1).to_broadcast([16, 8, width // 4])
+            rows = source[0].bitcast(I32).unsqueeze(1).to_broadcast([P // BLOCK, BLOCK, width // 4])
             nc.scalar.dma_start(tile[:].bitcast(I32), rows)
             return tile
 
@@ -57,9 +62,9 @@ def tile_picked_codeprodkindd_none_po_kernel(
         nc.sync.dma_start(x_table[:].bitcast(I32), x_words[0].rearrange("p c r -> p (c r)").bitcast(I32))
         n1_list = load_list(n1, "n1_list")
         n2_list = load_list(n2, "n2_list")
+        n3_list = load_list(n3, "n3_list")
         d_table = tables.tile([P, G], U32, name="d_table", offset=0)
         nc.sync.dma_start(d_table[:].bitcast(I32), d_words[0].rearrange("p c r -> p (c r)").bitcast(I32))
-        n3_list = load_list(n3, "n3_list")
         n4_list = load_list(n4, "n4_list")
         k2_list = load_list(k2, "k2_list")
         gains = keep.tile([P, PACK], F32, name="gains")
@@ -80,9 +85,11 @@ def tile_picked_codeprodkindd_none_po_kernel(
         def place_rows(spread, width, name, queues):
             placed = keep.tile([P, width], U8, name=name, align_bytes=64)
             nc.vector.memset(placed[:].bitcast(I32), 0)
-            for q in range(4):
+            for q in range(P // QUADRANT):
+                base = QUADRANT * q
                 queues[q % len(queues)].dma_start(
-                    placed[32 * q : 32 * q + 4, :].bitcast(I32), spread[32 * q : 32 * q + 32 : 8, :].bitcast(I32)
+                    placed[base : base + QUADRANT // BLOCK, :].bitcast(I32),
+                    spread[base : base + QUADRANT : BLOCK, :].bitcast(I32),
                 )
             return placed
 
@@ -94,8 +101,8 @@ def tile_picked_codeprodkindd_none_po_kernel(
         def deal_words(picked, name):
             dealt = keep.tile([P, H], U32, name=name, align_bytes=64)
             nc.vector.tensor_copy(
-                dealt[:].bitcast(I32).rearrange("p (t b i) -> p b t i", t=PACK, i=4),
-                picked[:].bitcast(I32).rearrange("p (b i t) -> p b t i", t=PACK, i=4),
+                dealt[:].bitcast(I32).rearrange("p (t b i) -> p b t i", t=PACK, i=LINE),
+                picked[:].bitcast(I32).rearrange("p (b i t) -> p b t i", t=PACK, i=LINE),
             )
             return dealt
 
@@ -161,7 +168,7 @@ def tile_picked_codeprodkindd_none_po_kernel(
             cols = slice(first, first + count)
             z_rounded = keep.tile([P, count, PACK], BF16, name=f"z_rounded{first}", align_bytes=64)
             nc.scalar.copy(
-                z_rounded[:].rearrange("p (c i) t -> p c t i", i=4), z.rearrange("p t (c i) -> p c t i", i=4)
+                z_rounded[:].rearrange("p (c i) t -> p c t i", i=LINE), z.rearrange("p t (c i) -> p c t i", i=LINE)
             )
             nc.vector.quantize_mx(
                 out=z_words[:, cols].bitcast(FP8X4),
@@ -184,20 +191,20 @@ def tile_picked_codeprodkindd_none_po_kernel(
                 )
                 nc.scalar.activation(h2[t][:, cols], banks2[t][:, cols], ACT.Copy, scale=SIXTEENTH)
 
-        most = S - QUARTER
-        z_rows = keep.tile([P, PACK + 2, most], F32, name="z_rows")
-        z_a = z_rows[:, 2 : PACK + 2, :]
-        left_a = [turns.tile([P, most], F32, name=f"left_a{t}", offset=(18 + 2 * t) * KIB) for t in range(PACK)]
-        gather_z(0, most, [tile[:] for tile in left_a], z_a)
-        quantise_z(0, HALF, z_a[:, :, 0:HALF])
+        work = keep.tile([P, PACK + 2, MOST], F32, name="work")
+        z_most = work[:, 2 : PACK + 2, :]
+        left_most = [factors.tile([P, MOST], F32, name=f"left_most{t}", offset=LEFT_BYTES * t) for t in range(PACK)]
+        gather_z(0, MOST, [tile[:] for tile in left_most], z_most)
+        quantise_z(0, HALF, z_most[:, :, 0:HALF])
         second_product(0)
-        quantise_z(HALF, QUARTER, z_a[:, :, HALF:most])
+        quantise_z(HALF, QUARTER, z_most[:, :, HALF:MOST])
 
-        z_c = z_rows[:, 0:PACK, 0:QUARTER]
-        left_c0 = turns.tile([P, QUARTER], F32, name="left_c0", offset=22 * KIB)
-        left_c12 = turns.tile([P, 2, QUARTER], F32, name="left_c12", offset=24 * KIB)
-        gather_z(most, QUARTER, [left_c0[:], left_c12[:, 0, :], left_c12[:, 1, :], z_rows[:, PACK, 0:QUARTER]], z_c)
-        quantise_z(most, QUARTER, z_c)
+        z_last = work[:, 0:PACK, 0:QUARTER]
+        left_last0 = factors.tile([P, QUARTER], F32, name="left_last0", offset=LEFT_BYTES * 2)
+        left_last12 = factors.tile([P, 2, QUARTER], F32, name="left_last12", offset=LEFT_BYTES * 3)
+        left_last = [left_last0[:], left_last12[:, 0, :], left_last12[:, 1, :], work[:, PACK, 0:QUARTER]]
+        gather_z(MOST, QUARTER, left_last, z_last)
+        quantise_z(MOST, QUARTER, z_last)
         second_product(HALF)
 
         y_words = keep.tile([P, S], U32, name="y_words", align_bytes=64)
@@ -214,8 +221,9 @@ def tile_picked_codeprodkindd_none_po_kernel(
                     ALU.subtract,
                 )
 
-        def make_y(first, count, partial, signed, last):
+        def make_y(first, count, partial, last):
             cols = slice(first, first + count)
+            signed = keep.tile([P, PACK, count], F32, name=f"signed{first}")
             y = keep.tile([P, PACK, count], F32, name=f"y{first}")
             for t in range(PACK):
                 nc.vector.tensor_tensor(
@@ -225,8 +233,8 @@ def tile_picked_codeprodkindd_none_po_kernel(
                     nc.scalar.activation(y[:, t, :], signed[:, t, :], ACT.Abs)
             y_rounded = keep.tile([P, count, PACK], BF16, name=f"y_rounded{first}", align_bytes=64)
             nc.scalar.activation(
-                y_rounded[:].rearrange("p (c i) t -> p c t i", i=4),
-                signed[:].rearrange("p t (c i) -> p c t i", i=4),
+                y_rounded[:].rearrange("p (c i) t -> p c t i", i=LINE),
+                signed[:].rearrange("p t (c i) -> p c t i", i=LINE),
                 ACT.Abs,
             )
             nc.scalar.activation(y[:, PACK - 1, :], signed[:, PACK - 1, :], ACT.Abs)
@@ -245,24 +253,26 @@ def tile_picked_codeprodkindd_none_po_kernel(
                 in_=y_rounded[:].rearrange("p c t -> p (c t)"),
             )
 
-        partial_a01 = keep.tile([P, 2, HALF], F32, name="partial_a01")
-        partial_a = [partial_a01[:, 0, :], partial_a01[:, 1, :], z_rows[:, 0, 0:HALF], z_rows[:, 1, 0:HALF]]
-        tab_less_h2(0, partial_a)
-        signed_a = keep.tile([P, PACK, HALF], F32, name="signed_a")
-        rounded_a = make_y(0, HALF, partial_a, signed_a, False)
+        partial_first01 = keep.tile([P, 2, HALF], F32, name="partial_first01")
+        partial_first = [partial_first01[:, 0, :], partial_first01[:, 1, :], work[:, 0, 0:HALF], work[:, 1, 0:HALF]]
+        tab_less_h2(0, partial_first)
+        rounded_first = make_y(0, HALF, partial_first, False)
 
-        z_flat = z_rows[:].rearrange("p r c -> p (r c)")
-        partial_b = [z_flat[:, HALF * t : HALF * (t + 1)] for t in range(PACK)]
-        tab_less_h2(HALF, partial_b)
-        signed_b = keep.tile([P, PACK, QUARTER], F32, name="signed_b")
-        rounded_b = make_y(HALF, QUARTER, [part[:, 0:QUARTER] for part in partial_b], signed_b, False)
-        signed_c = keep.tile([P, PACK, QUARTER], F32, name="signed_c")
-        rounded_c = make_y(HALF + QUARTER, QUARTER, [part[:, QUARTER:HALF] for part in partial_b], signed_c, True)
-        quantise_y(0, HALF, rounded_a)
-        quantise_y(HALF, QUARTER, rounded_b)
-        nc.sync.dma_start(out_words[:, 0:most], y_words[:, 0:most].bitcast(I32))
-        quantise_y(most, QUARTER, rounded_c)
-        nc.sync.dma_start(out_words[:, most:S], y_words[:, most:S].bitcast(I32))
-        for q in range(4):
+        work_flat = work[:].rearrange("p r c -> p (r c)")
+        partial_second = [work_flat[:, HALF * t : HALF * (t + 1)] for t in range(PACK)]
+        tab_less_h2(HALF, partial_second)
+        rounded_third = make_y(HALF, QUARTER, [part[:, 0:QUARTER] for part in partial_second], False)
+        rounded_last = make_y(MOST, QUARTER, [part[:, QUARTER:HALF] for part in partial_second], True)
+
+        quantise_y(0, HALF, rounded_first)
+        quantise_y(HALF, QUARTER, rounded_third)
+        nc.sync.dma_start(out_words[:, 0:MOST], y_words[:, 0:MOST].bitcast(I32))
+        quantise_y(MOST, QUARTER, rounded_last)
+        nc.sync.dma_start(out_words[:, MOST:S], y_words[:, MOST:S].bitcast(I32))
+        live = QUADRANT // BLOCK
+        for q in range(P // QUADRANT):
             queue = nc.sync if q % 2 == 0 else nc.scalar
-            queue.dma_start(out_2[0, 4 * q : 4 * q + 4, :].bitcast(I32), y_scales[32 * q : 32 * q + 4, :].bitcast(I32))
+            queue.dma_start(
+                out_2[0, live * q : live * (q + 1), :].bitcast(I32),
+                y_scales[QUADRANT * q : QUADRANT * q + live, :].bitcast(I32),
+            )

from contextlib import ExitStack

import concourse.mybir as mybir

K, T, S, G, H = 512, 1024, 512, 2048, 512
FLOPS = 2 * (2 * K * H * S)

F32 = mybir.dt.float32
BF16 = mybir.dt.bfloat16
I32 = mybir.dt.int32
U32 = mybir.dt.uint32
U16 = mybir.dt.uint16
U8 = mybir.dt.uint8
FP8X4 = mybir.dt.float8_e4m3fn_x4
ALU = mybir.AluOpType
ACT = mybir.ActivationFunctionType

P = 128
PACK = 4
GROUP = 16
BLOCK = 8
QUADRANT = 32
LINE = 4
SIXTEENTH = 0.0625
HALF = S // 2
QUARTER = S // 4
MOST = S - QUARTER
LEFT_BYTES = 2048


def tile_picked_codeprodkindd_none_po_kernel(
    tc, x_words, x_scales, d_words, d_scales, gs, tab, offs, k1, n1, n2, k2, n3, n4, out_0, out_1, out_2
):
    nc = tc.nc

    with ExitStack() as ctx:
        lists = ctx.enter_context(tc.tile_pool(name="lists", bufs=1))
        tables = ctx.enter_context(tc.tile_pool(name="tables", bufs=1))
        factors = ctx.enter_context(tc.tile_pool(name="factors", bufs=1))
        keep = ctx.enter_context(tc.tile_pool(name="keep", bufs=1))
        psum = ctx.enter_context(tc.psum_pool(name="psum", bufs=1))

        def load_list(source, name):
            tile = lists.tile([P, S // GROUP], U16, name=name)
            nc.sync.dma_start(tile[:], source)
            return tile

        def entries(tile, first, count):
            return tile[:, first // GROUP : (first + count) // GROUP]

        def load_scale_rows(source, width, name):
            tile = keep.tile([P, width], U8, name=name)
            rows = source[0].bitcast(I32).unsqueeze(1).to_broadcast([P // BLOCK, BLOCK, width // 4])
            nc.scalar.dma_start(tile[:].bitcast(I32), rows)
            return tile

        x_list = load_list(offs, "x_list")
        x_bytes = load_scale_rows(x_scales, T, "x_bytes")
        k1_list = load_list(k1, "k1_list")
        d_bytes = load_scale_rows(d_scales, G, "d_bytes")
        x_table = keep.tile([P, T], U32, name="x_table")
        nc.sync.dma_start(x_table[:].bitcast(I32), x_words[0].rearrange("p c r -> p (c r)").bitcast(I32))
        n1_list = load_list(n1, "n1_list")
        n2_list = load_list(n2, "n2_list")
        n3_list = load_list(n3, "n3_list")
        d_table = tables.tile([P, G], U32, name="d_table", offset=0)
        nc.sync.dma_start(d_table[:].bitcast(I32), d_words[0].rearrange("p c r -> p (c r)").bitcast(I32))
        n4_list = load_list(n4, "n4_list")
        k2_list = load_list(k2, "k2_list")
        gains = keep.tile([P, PACK], F32, name="gains")
        nc.sync.dma_start(gains[:], gs.rearrange("(p t) o -> p (t o)", t=PACK))
        gains16 = keep.tile([P, PACK], F32, name="gains16")
        nc.scalar.activation(gains16[:], gains[:], ACT.Copy, scale=SIXTEENTH)

        def gather_bytes(table, code_list, name):
            picked = keep.tile([P, S], U8, name=name)
            nc.vector.tensor_copy(picked[:], table[:].indirect(code_list[:]))
            return picked

        def deal_bytes(dealt, picked):
            nc.vector.tensor_copy(
                dealt.rearrange("p (t m) -> p t m", t=PACK), picked[:].rearrange("p (m t) -> p t m", t=PACK)
            )

        def place_rows(spread, width, name, queues):
            placed = keep.tile([P, width], U8, name=name, align_bytes=64)
            nc.vector.memset(placed[:].bitcast(I32), 0)
            for q in range(P // QUADRANT):
                base = QUADRANT * q
                queues[q % len(queues)].dma_start(
                    placed[base : base + QUADRANT // BLOCK, :].bitcast(I32),
                    spread[base : base + QUADRANT : BLOCK, :].bitcast(I32),
                )
            return placed

        def gather_words(table, code_list, name):
            picked = keep.tile([P, S], U32, name=name, align_bytes=64)
            nc.vector.tensor_copy(picked[:], table[:].indirect(code_list[:]))
            return picked

        def deal_words(picked, name):
            dealt = keep.tile([P, H], U32, name=name, align_bytes=64)
            nc.vector.tensor_copy(
                dealt[:].bitcast(I32).rearrange("p (t b i) -> p b t i", t=PACK, i=LINE),
                picked[:].bitcast(I32).rearrange("p (b i t) -> p b t i", t=PACK, i=LINE),
            )
            return dealt

        x_picked_bytes = gather_bytes(x_bytes, x_list, "x_picked_bytes")
        w1_bytes = gather_bytes(d_bytes, k1_list, "w1_bytes")
        spread1 = keep.tile([P, H + S], U8, name="spread1")
        nc.vector.tensor_copy(spread1[:, H : H + S].bitcast(I32), x_picked_bytes[:].bitcast(I32))
        deal_bytes(spread1[:, 0:H], w1_bytes)
        scales1 = place_rows(spread1, H + S, "scales1", (nc.scalar, nc.sync))

        x_picked = gather_words(x_table, x_list, "x_picked")
        w1_words = deal_words(gather_words(d_table, k1_list, "w1_picked"), "w1_words")

        banks1 = [psum.tile([P, S], F32, name=f"bank1_{t}") for t in range(PACK)]
        for t in range(PACK):
            rows = slice(P * t, P * (t + 1))
            nc.tensor.matmul_mx(
                out=banks1[t][:],
                lhsT=w1_words[:, rows].bitcast(FP8X4),
                lhsT_scale=scales1[:, rows],
                rhs=x_picked[:].bitcast(FP8X4),
                rhs_scale=scales1[:, H : H + S],
                start=True,
                stop=True,
            )

        w2_bytes = gather_bytes(d_bytes, k2_list, "w2_bytes")
        w2_picked = gather_words(d_table, k2_list, "w2_picked")
        spread2 = keep.tile([P, H], U8, name="spread2")
        deal_bytes(spread2[:], w2_bytes)
        w2_scales = place_rows(spread2, H, "w2_scales", (nc.sync,))
        w2_words = deal_words(w2_picked, "w2_words")

        tabs = [tables.tile([P, S], F32, name=f"tab{t}", offset=4 * S * t) for t in range(PACK)]
        tab_rows = tab.rearrange("(p t) j -> p t j", t=PACK)
        for t in range(PACK):
            nc.sync.dma_start(tabs[t][:], tab_rows[:, t, :])

        h_gained = [keep.tile([P, S], F32, name=f"h_gained{t}") for t in range(PACK)]
        h_plain = [keep.tile([P, S], F32, name=f"h_plain{t}") for t in range(PACK)]
        for step in range(PACK + 1):
            if step < PACK:
                nc.scalar.activation(h_gained[step][:], banks1[step][:], ACT.Copy, scale=gains16[:, step : step + 1])
            if step > 0:
                nc.scalar.activation(h_plain[step - 1][:], banks1[step - 1][:], ACT.Copy, scale=SIXTEENTH)

        z_words = keep.tile([P, S], U32, name="z_words", align_bytes=64)
        z_scales = keep.tile([P, S], U8, name="z_scales", align_bytes=64)
        banks2 = [psum.tile([P, S], F32, name=f"bank2_{t}") for t in range(PACK)]
        h2 = [keep.tile([P, S], F32, name=f"h2_{t}") for t in range(PACK)]

        def gather_z(first, count, left, z):
            for step in range(PACK + 1):
                if step < PACK:
                    nc.vector.tensor_copy(left[step], h_gained[step][:].indirect(entries(n1_list, first, count)))
                if step > 0:
                    t = step - 1
                    nc.vector.tensor_tensor(
                        z[:, t, :], h_plain[t][:].indirect(entries(n2_list, first, count)), left[t], ALU.mult
                    )

        def quantise_z(first, count, z):
            cols = slice(first, first + count)
            z_rounded = keep.tile([P, count, PACK], BF16, name=f"z_rounded{first}", align_bytes=64)
            nc.scalar.copy(
                z_rounded[:].rearrange("p (c i) t -> p c t i", i=LINE), z.rearrange("p t (c i) -> p c t i", i=LINE)
            )
            nc.vector.quantize_mx(
                out=z_words[:, cols].bitcast(FP8X4),
                scales=z_scales[:, cols],
                in_=z_rounded[:].rearrange("p c t -> p (c t)"),
            )

        def second_product(first):
            cols = slice(first, first + HALF)
            for t in range(PACK):
                rows = slice(P * t, P * (t + 1))
                nc.tensor.matmul_mx(
                    out=banks2[t][:, cols],
                    lhsT=w2_words[:, rows].bitcast(FP8X4),
                    lhsT_scale=w2_scales[:, rows],
                    rhs=z_words[:, cols].bitcast(FP8X4),
                    rhs_scale=z_scales[:, cols],
                    start=True,
                    stop=True,
                )
                nc.scalar.activation(h2[t][:, cols], banks2[t][:, cols], ACT.Copy, scale=SIXTEENTH)

        work = keep.tile([P, PACK + 2, MOST], F32, name="work")
        z_most = work[:, 2 : PACK + 2, :]
        left_most = [factors.tile([P, MOST], F32, name=f"left_most{t}", offset=LEFT_BYTES * t) for t in range(PACK)]
        gather_z(0, MOST, [tile[:] for tile in left_most], z_most)
        quantise_z(0, HALF, z_most[:, :, 0:HALF])
        second_product(0)
        quantise_z(HALF, QUARTER, z_most[:, :, HALF:MOST])

        z_last = work[:, 0:PACK, 0:QUARTER]
        left_last0 = factors.tile([P, QUARTER], F32, name="left_last0", offset=LEFT_BYTES * 2)
        left_last12 = factors.tile([P, 2, QUARTER], F32, name="left_last12", offset=LEFT_BYTES * 3)
        left_last = [left_last0[:], left_last12[:, 0, :], left_last12[:, 1, :], work[:, PACK, 0:QUARTER]]
        gather_z(MOST, QUARTER, left_last, z_last)
        quantise_z(MOST, QUARTER, z_last)
        second_product(HALF)

        y_words = keep.tile([P, S], U32, name="y_words", align_bytes=64)
        y_scales = keep.tile([P, S], U8, name="y_scales", align_bytes=64)
        out_rows = out_0.rearrange("(p t) j -> p t j", t=PACK)
        out_words = out_1[0].rearrange("p c r -> p (c r)").bitcast(I32)

        def tab_less_h2(first, partial):
            for t in range(PACK):
                nc.vector.tensor_tensor(
                    partial[t],
                    tabs[t][:].indirect(entries(n3_list, first, HALF)),
                    h2[t][:, first : first + HALF],
                    ALU.subtract,
                )

        def make_y(first, count, partial, last):
            cols = slice(first, first + count)
            signed = keep.tile([P, PACK, count], F32, name=f"signed{first}")
            y = keep.tile([P, PACK, count], F32, name=f"y{first}")
            for t in range(PACK):
                nc.vector.tensor_tensor(
                    signed[:, t, :], h2[t][:].indirect(entries(n4_list, first, count)), partial[t], ALU.add
                )
                if t < PACK - 1:
                    nc.scalar.activation(y[:, t, :], signed[:, t, :], ACT.Abs)
            y_rounded = keep.tile([P, count, PACK], BF16, name=f"y_rounded{first}", align_bytes=64)
            nc.scalar.activation(
                y_rounded[:].rearrange("p (c i) t -> p c t i", i=LINE),
                signed[:].rearrange("p t (c i) -> p c t i", i=LINE),
                ACT.Abs,
            )
            nc.scalar.activation(y[:, PACK - 1, :], signed[:, PACK - 1, :], ACT.Abs)
            if last:
                nc.sync.dma_start(out_rows[:, 0 : PACK - 1, cols], y[:, 0 : PACK - 1, :])
                nc.scalar.dma_start(out_rows[:, PACK - 1, cols], y[:, PACK - 1, :])
            else:
                nc.sync.dma_start(out_rows[:, :, cols], y[:])
            return y_rounded

        def quantise_y(first, count, y_rounded):
            cols = slice(first, first + count)
            nc.vector.quantize_mx(
                out=y_words[:, cols].bitcast(FP8X4),
                scales=y_scales[:, cols],
                in_=y_rounded[:].rearrange("p c t -> p (c t)"),
            )

        partial_first01 = keep.tile([P, 2, HALF], F32, name="partial_first01")
        partial_first = [partial_first01[:, 0, :], partial_first01[:, 1, :], work[:, 0, 0:HALF], work[:, 1, 0:HALF]]
        tab_less_h2(0, partial_first)
        rounded_first = make_y(0, HALF, partial_first, False)

        work_flat = work[:].rearrange("p r c -> p (r c)")
        partial_second = [work_flat[:, HALF * t : HALF * (t + 1)] for t in range(PACK)]
        tab_less_h2(HALF, partial_second)
        rounded_third = make_y(HALF, QUARTER, [part[:, 0:QUARTER] for part in partial_second], False)
        rounded_last = make_y(MOST, QUARTER, [part[:, QUARTER:HALF] for part in partial_second], True)

        quantise_y(0, HALF, rounded_first)
        quantise_y(HALF, QUARTER, rounded_third)
        nc.sync.dma_start(out_words[:, 0:MOST], y_words[:, 0:MOST].bitcast(I32))
        quantise_y(MOST, QUARTER, rounded_last)
        nc.sync.dma_start(out_words[:, MOST:S], y_words[:, MOST:S].bitcast(I32))
        live = QUADRANT // BLOCK
        for q in range(P // QUADRANT):
            queue = nc.sync if q % 2 == 0 else nc.scalar
            queue.dma_start(
                out_2[0, live * q : live * (q + 1), :].bitcast(I32),
                y_scales[QUADRANT * q : QUADRANT * q + live, :].bitcast(I32),
            )
